import numpy as np
import ml_dtypes


def mxq(x, axis, fmt="e4m3"):
    dtype, down = {"e4m3": (ml_dtypes.float8_e4m3fn, 7), "e5m2": (ml_dtypes.float8_e5m2, 14)}[fmt]
    v = np.moveaxis(np.asarray(x, np.float32).astype(ml_dtypes.bfloat16).astype(np.float64), axis, -1)
    blocks = v.reshape(v.shape[:-1] + (-1, 32))
    amax = np.abs(blocks).max(-1, keepdims=True)
    byte = np.maximum(np.where(amax > 0, np.frexp(amax)[1] - 1 + 127, 0) - down, 1)
    scale = np.exp2(byte - 127.0)
    codes = (blocks / scale).astype(np.float32).astype(dtype).astype(np.float64)
    return np.moveaxis((codes * scale).reshape(v.shape), -1, axis)


WIDE = False


def mx_kscale(k):
    if not WIDE:
        return np.ones(k)
    levels = np.array([10, -10, 5, -5, 0])
    if k % 512:
        return np.exp2(np.random.permutation(np.resize(levels, k // 32))).repeat(32)
    a = np.empty((k // 512, 16))
    for p in range(k // 512):
        a[p, :8] = np.random.permutation(np.resize(levels, 8))
        for g in range(8):
            far = levels[np.abs(levels - a[p, g]) >= 10]
            a[p, g + 8] = far[np.random.randint(len(far))]
    return np.exp2(a.ravel()).repeat(32)


def f64(x):
    return np.asarray(x).astype(np.float64)


def striped(idx):
    return np.tile(np.asarray(idx).reshape(-1, 16).T, (8, 1)).astype(np.uint16)


def unstriped(offs):
    return offs[:16].T.reshape(-1).astype(np.int64)


E2M1 = np.array([0.0, 0.5, 1.0, 1.5, 2.0, 3.0, 4.0, 6.0, -0.0, -0.5, -1.0, -1.5, -2.0, -3.0, -4.0, -6.0])


def pack_weight(w, fmt):
    k, n = w.shape
    w = f64(np.asarray(w, np.float32).astype(ml_dtypes.bfloat16)).reshape(k // 32, 32, n)
    amax = np.abs(w).max(1)
    if fmt == "e4m3":
        byte = np.frexp(amax)[1] - 1 + 127 - 7
    else:
        mant, ex = np.frexp(amax / 6.0)
        byte = np.where(mant > 0.5, ex, ex - 1) + 127
    byte = np.clip(np.where(amax > 0, byte, 1), 1, 254)
    scaled = (w * np.exp2(127.0 - byte)[:, None, :]).reshape(k, n).astype(np.float32)
    by_word = np.ascontiguousarray(scaled.reshape(k // 512, 128, 4, n).transpose(0, 1, 3, 2))
    if fmt == "e4m3":
        words = by_word.astype(ml_dtypes.float8_e4m3fn).view(np.uint8)
    else:
        c = by_word.astype(ml_dtypes.float4_e2m1fn).view(np.uint8) & 0xF
        words = (c[..., 0::2] | (c[..., 1::2] << 4)).reshape(k // 512, 128, 2 * n)
    return np.ascontiguousarray(words), np.ascontiguousarray(byte.astype(np.uint8).reshape(k // 512, 16, n))


def unpack_weight(words, scales, fmt):
    g, _, n = scales.shape
    words = np.ascontiguousarray(words).reshape(g, 128, n, -1)
    if fmt == "e4m3":
        vals = words.view(ml_dtypes.float8_e4m3fn).astype(np.float64)
    else:
        nib = np.empty((g, 128, n, 4), np.uint8)
        nib[..., 0::2] = words & 0xF
        nib[..., 1::2] = words >> 4
        vals = E2M1[nib]
    vals = vals * np.repeat(np.exp2(scales.astype(np.float64) - 127.0), 8, axis=1)[..., None]
    return vals.transpose(0, 1, 3, 2).reshape(g * 512, n)


D, K, T, M, I, E = 512, 512, 2048, 1024, 512, 256


def setup_inputs():
    n = np.random.standard_normal
    idx = np.random.permutation(T)[:I]
    idx2 = np.random.permutation(M)[:I]
    idx3 = np.random.permutation(M)[:I]
    fd = mx_kscale(D)
    fk = mx_kscale(K)
    pagesp = pack_weight(n((D, T)) / fd[:, None], "e4m3")
    wap = pack_weight(n((D, K)) * 1.0 / np.sqrt(D) * fd[:, None], "e2m1")
    wop = pack_weight(n((K, E)) * 1.0 / np.sqrt(K) / fk[:, None], "e2m1")
    return {
        "pages_words": pagesp[0],
        "pages_scales": pagesp[1],
        "wa_words": wap[0],
        "wa_scales": wap[1],
        "kf": (np.random.uniform(0.5, 2.0, (K, 1)) * fk[:, None]).astype(np.float32),
        "wo_words": wop[0],
        "wo_scales": wop[1],
        "store": (1.0 * n((E, M))).astype(np.float32),
        "offs": striped(idx),
        "offs2": striped(idx2),
        "offs3": striped(idx3),
    }


def reference(pages_words, pages_scales, wa_words, wa_scales, kf, wo_words, wo_scales, store, offs, offs2, offs3):
    idx = unstriped(offs)
    idx2 = unstriped(offs2)
    idx3 = unstriped(offs3)
    pagesu = unpack_weight(pages_words, pages_scales, "e4m3")
    wau = unpack_weight(wa_words, wa_scales, "e2m1")
    wou = unpack_weight(wo_words, wo_scales, "e2m1")
    pagesidxg = pagesu[:, idx]
    z = wau.T @ pagesidxg
    w = z * f64(kf)
    wq = mxq(w, 0, "e4m3")
    o = wou.T @ wq
    f1 = np.zeros((E, M))
    f1[:, idx2] = o
    c1 = f64(store) + f1
    y = c1[:, idx3] - o
    return y

@@ -1,0 +1,163 @@
+from contextlib import ExitStack
+
+import concourse.mybir as mybir
+
+F32 = mybir.dt.float32
+BF16 = mybir.dt.bfloat16
+I32 = mybir.dt.int32
+U32 = mybir.dt.uint32
+U16 = mybir.dt.uint16
+U8 = mybir.dt.uint8
+FP8X4 = mybir.dt.float8_e4m3fn_x4
+FP4X4 = mybir.dt.float4_e2m1fn_x4
+COPY = mybir.ActivationFunctionType.Copy
+MULT = mybir.AluOpType.mult
+ADD = mybir.AluOpType.add
+SUBTRACT = mybir.AluOpType.subtract
+
+P = 128
+PACK = 4
+D, K, T, M, SLOTS, E = 512, 512, 2048, 1024, 512, 256
+CHUNK = 128
+CHUNKS = SLOTS // CHUNK
+HALF = SLOTS // 2
+FLOPS = 2 * D * K * SLOTS + 2 * K * E * SLOTS
+
+
+def entries(offsets, start, count):
+    return offsets[:, start // 16 : (start + count) // 16]
+
+
+def load_scale_rows(queue, tile, rows, quadrants):
+    for q in quadrants:
+        queue.dma_start(tile[32 * q : 32 * q + 4, :].bitcast(I32), rows[0, 4 * q : 4 * q + 4, :].bitcast(I32))
+
+
+def tile_attend_outputsback_kernel(tc, pages_words, pages_scales, wa_words, wa_scales, kf, wo_words, wo_scales,
+                                    store, offs, offs2, offs3, out):
+    nc = tc.nc
+    with ExitStack() as ctx:
+        sb = ctx.enter_context(tc.tile_pool(name="sb", bufs=1))
+        psum = ctx.enter_context(tc.psum_pool(name="psum", bufs=1))
+
+        idx = sb.tile([P, SLOTS // 16], U16, name="idx")
+        idx2 = sb.tile([P, SLOTS // 16], U16, name="idx2")
+        idx3 = sb.tile([P, SLOTS // 16], U16, name="idx3")
+        page_words = sb.tile([P, T], I32, name="page_words", align_bytes=64)
+        page_scales = sb.tile([P, T], U8, name="page_scales", align_bytes=64)
+        wa_raw = sb.tile([P, 2 * K], U8, name="wa_raw", align_bytes=64)
+        wa_raw_scales = sb.tile([P, K], U8, name="wa_raw_scales", align_bytes=64)
+        wa_codes = sb.tile([P, 2 * K], U8, name="wa_codes", align_bytes=64)
+        wa_plane = sb.tile([P, K], U8, name="wa_plane", align_bytes=64)
+        wo_codes = sb.tile([P, 2 * E], U8, name="wo_codes", align_bytes=64)
+        wo_plane = sb.tile([P, E], U8, name="wo_plane", align_bytes=64)
+        factors = sb.tile([P, 1, PACK], F32, name="factors")
+        picked_words = sb.tile([P, SLOTS], U32, name="picked_words", align_bytes=64)
+        picked_scales = sb.tile([P, SLOTS], U8, name="picked_scales", align_bytes=64)
+        w_codes = sb.tile([P, SLOTS], U32, name="w_codes", align_bytes=64)
+        w_plane = sb.tile([P, SLOTS], U8, name="w_plane", align_bytes=64)
+        o_early = sb.tile([P, 2, HALF], F32, name="o_early", align_bytes=64)
+        o_late = sb.tile([P, 2, HALF], F32, name="o_late", align_bytes=64)
+        old = [sb.tile([P, M], F32, name="old%d" % h, tag="old%d" % h, align_bytes=64) for h in range(2)]
+        placed = [sb.tile([P, M], F32, name="placed%d" % h, align_bytes=64) for h in range(2)]
+        looked0 = sb.tile([P, SLOTS], F32, name="looked0", align_bytes=64)
+        looked1 = sb.tile([P, HALF], F32, name="looked1", align_bytes=64)
+        res0 = sb.tile([P, SLOTS], F32, name="res0", align_bytes=64)
+        res1a = sb.tile([P, HALF], F32, name="res1a", align_bytes=64)
+        res1b = sb.tile([P, HALF], F32, name="res1b", align_bytes=64)
+
+        nc.vector.memset(page_scales[:].bitcast(I32), 0)
+        nc.vector.memset(wa_raw_scales[:].bitcast(I32), 0)
+        nc.vector.memset(wo_plane[:].bitcast(I32), 0)
+        for h in range(2):
+            nc.vector.memset(placed[h][:], 0.0)
+
+        nc.sync.dma_start(idx[:], offs)
+        nc.sync.dma_start(wa_raw[:].bitcast(I32), wa_words[0].bitcast(I32))
+        load_scale_rows(nc.sync, page_scales, pages_scales, range(4))
+        nc.sync.dma_start(page_words[:], pages_words[0].rearrange("p n t -> p (n t)").bitcast(I32))
+        nc.sync.dma_start(factors[:], kf.rearrange("(p t) u -> p u t", t=PACK))
+        load_scale_rows(nc.sync, wa_raw_scales, wa_scales, range(4))
+        nc.sync.dma_start(wo_codes[:].bitcast(I32), wo_words[0].bitcast(I32))
+        load_scale_rows(nc.sync, wo_plane, wo_scales, range(4))
+        nc.sync.dma_start(idx2[:], offs2)
+        for h in range(2):
+            nc.sync.dma_start(old[h][:], store[h * P : (h + 1) * P, :])
+        nc.sync.dma_start(idx3[:], offs3)
+
+        nc.vector.tensor_copy(
+            wa_codes[:].bitcast(U16).rearrange("p (t m) -> p t m", t=PACK),
+            wa_raw[:].bitcast(U16).rearrange("p (m t) -> p t m", t=PACK),
+        )
+        nc.vector.tensor_copy(picked_scales[:], page_scales[:].indirect(idx[:]))
+        nc.vector.tensor_copy(
+            wa_plane[:].rearrange("p (t m) -> p t m", t=PACK),
+            wa_raw_scales[:].rearrange("p (m t) -> p t m", t=PACK),
+        )
+
+        z = []
+        for c in range(CHUNKS):
+            cols = slice(c * CHUNK, (c + 1) * CHUNK)
+            nc.vector.tensor_copy(picked_words[:, cols], page_words[:].bitcast(U32).indirect(entries(idx, c * CHUNK, CHUNK)))
+            bank = psum.tile([P, PACK, CHUNK], F32, name="z%d" % c)
+            for t in range(PACK):
+                nc.tensor.matmul_mx(
+                    bank[:, t, :],
+                    lhsT=wa_codes[:, 2 * P * t : 2 * P * (t + 1)].bitcast(FP4X4),
+                    lhsT_scale=wa_plane[:, P * t : P * (t + 1)],
+                    rhs=picked_words[:, cols].bitcast(FP8X4),
+                    rhs_scale=picked_scales[:, cols],
+                    start=True,
+                    stop=True,
+                )
+            z.append(bank)
+
+        def output_product(bank, cols):
+            for h in range(2):
+                nc.tensor.matmul_mx(
+                    bank[:, h, :],
+                    lhsT=wo_codes[:, 2 * P * h : 2 * P * (h + 1)].bitcast(FP4X4),
+                    lhsT_scale=wo_plane[:, P * h : P * (h + 1)],
+                    rhs=w_codes[:, cols].bitcast(FP8X4),
+                    rhs_scale=w_plane[:, cols],
+                    start=True,
+                    stop=True,
+                )
+
+        for c in range(CHUNKS):
+            cols = slice(c * CHUNK, (c + 1) * CHUNK)
+            w = sb.tile([P, CHUNK, PACK], BF16, name="w%d" % c, align_bytes=64)
+            nc.vector.tensor_tensor(
+                w[:], z[c][:].rearrange("p t i -> p i t"), factors[:].to_broadcast([P, CHUNK, PACK]), MULT
+            )
+            nc.vector.quantize_mx(
+                w_codes[:, cols].bitcast(FP8X4), w_plane[:, cols], w[:].rearrange("p i t -> p (i t)")
+            )
+            if c < 2:
+                bank = psum.tile([P, 2, CHUNK], F32, name="o%d" % c)
+                output_product(bank, cols)
+                nc.scalar.activation(o_early[:, :, cols], bank[:], COPY)
+        bank = psum.tile([P, 2, HALF], F32, name="o_late_bank")
+        output_product(bank, slice(HALF, SLOTS))
+
+        nc.scalar.activation(placed[0][:].indirect(entries(idx2, 0, HALF)), o_early[:, 0, :], COPY)
+        nc.vector.tensor_copy(placed[1][:].indirect(entries(idx2, 0, CHUNK)), o_early[:, 1, :CHUNK])
+        nc.vector.tensor_copy(o_late[:], bank[:])
+        nc.scalar.activation(placed[0][:].indirect(entries(idx2, HALF, HALF)), o_late[:, 0, :], COPY)
+        nc.vector.tensor_copy(placed[1][:].indirect(entries(idx2, HALF, HALF)), o_late[:, 1, :])
+        nc.scalar.activation(placed[1][:].indirect(entries(idx2, CHUNK, CHUNK)), o_early[:, 1, CHUNK:], COPY)
+
+        c1 = []
+        for h, tag in enumerate(("c1", "old0")):
+            c1.append(sb.tile([P, M], F32, name="c1_%d" % h, tag=tag, align_bytes=64))
+            nc.vector.tensor_tensor(c1[h][:], old[h][:], placed[h][:], ADD)
+
+        nc.scalar.activation(looked0[:], c1[0][:].indirect(idx3[:]), COPY)
+        nc.scalar.activation(looked1[:], c1[1][:].indirect(entries(idx3, 0, HALF)), COPY)
+        nc.vector.tensor_tensor(res1b[:], c1[1][:].indirect(entries(idx3, HALF, HALF)), o_late[:, 1, :], SUBTRACT)
+        nc.sync.dma_start(out[P:, HALF:], res1b[:])
+        nc.vector.tensor_tensor(res0[:, :HALF], looked0[:, :HALF], o_early[:, 0, :], SUBTRACT)
+        nc.vector.tensor_tensor(res0[:, HALF:], looked0[:, HALF:], o_late[:, 0, :], SUBTRACT)
+        nc.sync.dma_start(out[:P, :], res0[:])
+        nc.vector.tensor_tensor(res1a[:], looked1[:], o_early[:, 1, :], SUBTRACT)
+        nc.sync.dma_start(out[P:, :HALF], res1a[:])

@@ -46,13 +46,12 @@ def tile_attend_outputsback_kernel(tc, pages_words, pages_scales, wa_words, wa_s
         page_words = sb.tile([P, T], I32, name="page_words", align_bytes=64)
         page_scales = sb.tile([P, T], U8, name="page_scales", align_bytes=64)
         wa_raw = sb.tile([P, 2 * K], U8, name="wa_raw", align_bytes=64)
-        wa_raw_scales = sb.tile([P, K], U8, name="wa_raw_scales", align_bytes=64)
+        wa_raw_scales = sb.tile([P, K], U8, name="wa_raw_scales", tag="staged", align_bytes=64)
         wa_codes = sb.tile([P, 2 * K], U8, name="wa_codes", align_bytes=64)
         wa_plane = sb.tile([P, K], U8, name="wa_plane", align_bytes=64)
         wo_codes = sb.tile([P, 2 * E], U8, name="wo_codes", align_bytes=64)
         wo_plane = sb.tile([P, E], U8, name="wo_plane", align_bytes=64)
         factors = sb.tile([P, 1, PACK], F32, name="factors")
-        picked_words = sb.tile([P, SLOTS], U32, name="picked_words", align_bytes=64)
         picked_scales = sb.tile([P, SLOTS], U8, name="picked_scales", align_bytes=64)
         w_codes = sb.tile([P, SLOTS], U32, name="w_codes", align_bytes=64)
         w_plane = sb.tile([P, SLOTS], U8, name="w_plane", align_bytes=64)
@@ -73,16 +72,16 @@ def tile_attend_outputsback_kernel(tc, pages_words, pages_scales, wa_words, wa_s
             nc.vector.memset(placed[h][:], 0.0)
 
         nc.sync.dma_start(idx[:], offs)
-        nc.sync.dma_start(wa_raw[:].bitcast(I32), wa_words[0].bitcast(I32))
-        load_scale_rows(nc.sync, page_scales, pages_scales, range(4))
-        nc.sync.dma_start(page_words[:], pages_words[0].rearrange("p n t -> p (n t)").bitcast(I32))
         nc.sync.dma_start(factors[:], kf.rearrange("(p t) u -> p u t", t=PACK))
-        load_scale_rows(nc.sync, wa_raw_scales, wa_scales, range(4))
+        nc.sync.dma_start(wa_raw[:].bitcast(I32), wa_words[0].bitcast(I32))
+        nc.sync.dma_start(page_words[:], pages_words[0].rearrange("p n t -> p (n t)").bitcast(I32))
+        load_scale_rows(nc.scalar, page_scales, pages_scales, range(4))
+        load_scale_rows(nc.scalar, wa_raw_scales, wa_scales, range(4))
+        nc.sync.dma_start(old[0][:], store[:P, :])
         nc.sync.dma_start(wo_codes[:].bitcast(I32), wo_words[0].bitcast(I32))
         load_scale_rows(nc.sync, wo_plane, wo_scales, range(4))
         nc.sync.dma_start(idx2[:], offs2)
-        for h in range(2):
-            nc.sync.dma_start(old[h][:], store[h * P : (h + 1) * P, :])
+        nc.sync.dma_start(old[1][:], store[P:, :])
         nc.sync.dma_start(idx3[:], offs3)
 
         nc.vector.tensor_copy(
@@ -95,6 +94,7 @@ def tile_attend_outputsback_kernel(tc, pages_words, pages_scales, wa_words, wa_s
             wa_raw_scales[:].rearrange("p (m t) -> p t m", t=PACK),
         )
 
+        picked_words = sb.tile([P, SLOTS], U32, name="picked_words", tag="staged", align_bytes=64)
         z = []
         for c in range(CHUNKS):
             cols = slice(c * CHUNK, (c + 1) * CHUNK)
@@ -140,11 +140,11 @@ def tile_attend_outputsback_kernel(tc, pages_words, pages_scales, wa_words, wa_s
         bank = psum.tile([P, 2, HALF], F32, name="o_late_bank")
         output_product(bank, slice(HALF, SLOTS))
 
-        nc.scalar.activation(placed[0][:].indirect(entries(idx2, 0, HALF)), o_early[:, 0, :], COPY)
-        nc.vector.tensor_copy(placed[1][:].indirect(entries(idx2, 0, CHUNK)), o_early[:, 1, :CHUNK])
-        nc.vector.tensor_copy(o_late[:], bank[:])
-        nc.scalar.activation(placed[0][:].indirect(entries(idx2, HALF, HALF)), o_late[:, 0, :], COPY)
-        nc.vector.tensor_copy(placed[1][:].indirect(entries(idx2, HALF, HALF)), o_late[:, 1, :])
+        nc.vector.tensor_copy(placed[0][:].indirect(entries(idx2, 0, HALF)), o_early[:, 0, :])
+        nc.scalar.activation(placed[1][:].indirect(entries(idx2, 0, CHUNK)), o_early[:, 1, :CHUNK], COPY)
+        nc.scalar.activation(o_late[:], bank[:], COPY)
+        nc.vector.tensor_copy(placed[0][:].indirect(entries(idx2, HALF, HALF)), o_late[:, 0, :])
+        nc.scalar.activation(placed[1][:].indirect(entries(idx2, HALF, HALF)), o_late[:, 1, :], COPY)
         nc.scalar.activation(placed[1][:].indirect(entries(idx2, CHUNK, CHUNK)), o_early[:, 1, CHUNK:], COPY)
 
         c1 = []

@@ -21,6 +21,7 @@ D, K, T, M, SLOTS, E = 512, 512, 2048, 1024, 512, 256
 CHUNK = 128
 CHUNKS = SLOTS // CHUNK
 HALF = SLOTS // 2
+PLAIN = SLOTS - CHUNK
 FLOPS = 2 * D * K * SLOTS + 2 * K * E * SLOTS
 
 
@@ -57,13 +58,10 @@ def tile_attend_outputsback_kernel(tc, pages_words, pages_scales, wa_words, wa_s
         w_plane = sb.tile([P, SLOTS], U8, name="w_plane", align_bytes=64)
         o_early = sb.tile([P, 2, HALF], F32, name="o_early", align_bytes=64)
         o_late = sb.tile([P, 2, HALF], F32, name="o_late", align_bytes=64)
-        old = [sb.tile([P, M], F32, name="old%d" % h, tag="old%d" % h, align_bytes=64) for h in range(2)]
+        old = [sb.tile([P, M], F32, name="old%d" % h, align_bytes=64) for h in range(2)]
         placed = [sb.tile([P, M], F32, name="placed%d" % h, align_bytes=64) for h in range(2)]
-        looked0 = sb.tile([P, SLOTS], F32, name="looked0", align_bytes=64)
-        looked1 = sb.tile([P, HALF], F32, name="looked1", align_bytes=64)
-        res0 = sb.tile([P, SLOTS], F32, name="res0", align_bytes=64)
-        res1a = sb.tile([P, HALF], F32, name="res1a", align_bytes=64)
-        res1b = sb.tile([P, HALF], F32, name="res1b", align_bytes=64)
+        looked = [sb.tile([P, PLAIN], F32, name="looked%d" % h, align_bytes=64) for h in range(2)]
+        res = [sb.tile([P, SLOTS], F32, name="res%d" % h, align_bytes=64) for h in range(2)]
 
         nc.vector.memset(page_scales[:].bitcast(I32), 0)
         nc.vector.memset(wa_raw_scales[:].bitcast(I32), 0)
@@ -72,16 +70,16 @@ def tile_attend_outputsback_kernel(tc, pages_words, pages_scales, wa_words, wa_s
             nc.vector.memset(placed[h][:], 0.0)
 
         nc.sync.dma_start(idx[:], offs)
-        nc.sync.dma_start(factors[:], kf.rearrange("(p t) u -> p u t", t=PACK))
         nc.sync.dma_start(wa_raw[:].bitcast(I32), wa_words[0].bitcast(I32))
+        load_scale_rows(nc.sync, page_scales, pages_scales, range(4))
         nc.sync.dma_start(page_words[:], pages_words[0].rearrange("p n t -> p (n t)").bitcast(I32))
-        load_scale_rows(nc.scalar, page_scales, pages_scales, range(4))
-        load_scale_rows(nc.scalar, wa_raw_scales, wa_scales, range(4))
-        nc.sync.dma_start(old[0][:], store[:P, :])
+        nc.sync.dma_start(factors[:], kf.rearrange("(p t) u -> p u t", t=PACK))
+        load_scale_rows(nc.sync, wa_raw_scales, wa_scales, range(4))
         nc.sync.dma_start(wo_codes[:].bitcast(I32), wo_words[0].bitcast(I32))
         load_scale_rows(nc.sync, wo_plane, wo_scales, range(4))
         nc.sync.dma_start(idx2[:], offs2)
-        nc.sync.dma_start(old[1][:], store[P:, :])
+        for h in range(2):
+            nc.sync.dma_start(old[h][:], store[h * P : (h + 1) * P, :])
         nc.sync.dma_start(idx3[:], offs3)
 
         nc.vector.tensor_copy(
@@ -94,18 +92,20 @@ def tile_attend_outputsback_kernel(tc, pages_words, pages_scales, wa_words, wa_s
             wa_raw_scales[:].rearrange("p (m t) -> p t m", t=PACK),
         )
 
-        picked_words = sb.tile([P, SLOTS], U32, name="picked_words", tag="staged", align_bytes=64)
+        picked_first = sb.tile([P, CHUNK], U32, name="picked_first", align_bytes=64)
+        picked_rest = sb.tile([P, SLOTS - CHUNK], U32, name="picked_rest", tag="staged", align_bytes=64)
+        picked_words = [picked_first[:]] + [picked_rest[:, c * CHUNK : (c + 1) * CHUNK] for c in range(CHUNKS - 1)]
         z = []
         for c in range(CHUNKS):
             cols = slice(c * CHUNK, (c + 1) * CHUNK)
-            nc.vector.tensor_copy(picked_words[:, cols], page_words[:].bitcast(U32).indirect(entries(idx, c * CHUNK, CHUNK)))
+            nc.vector.tensor_copy(picked_words[c], page_words[:].bitcast(U32).indirect(entries(idx, c * CHUNK, CHUNK)))
             bank = psum.tile([P, PACK, CHUNK], F32, name="z%d" % c)
             for t in range(PACK):
                 nc.tensor.matmul_mx(
                     bank[:, t, :],
                     lhsT=wa_codes[:, 2 * P * t : 2 * P * (t + 1)].bitcast(FP4X4),
                     lhsT_scale=wa_plane[:, P * t : P * (t + 1)],
-                    rhs=picked_words[:, cols].bitcast(FP8X4),
+                    rhs=picked_words[c].bitcast(FP8X4),
                     rhs_scale=picked_scales[:, cols],
                     start=True,
                     stop=True,
@@ -148,16 +148,20 @@ def tile_attend_outputsback_kernel(tc, pages_words, pages_scales, wa_words, wa_s
         nc.scalar.activation(placed[1][:].indirect(entries(idx2, CHUNK, CHUNK)), o_early[:, 1, CHUNK:], COPY)
 
         c1 = []
-        for h, tag in enumerate(("c1", "old0")):
-            c1.append(sb.tile([P, M], F32, name="c1_%d" % h, tag=tag, align_bytes=64))
+        for h in range(2):
+            c1.append(sb.tile([P, M], F32, name="c1_%d" % h, align_bytes=64))
             nc.vector.tensor_tensor(c1[h][:], old[h][:], placed[h][:], ADD)
 
-        nc.scalar.activation(looked0[:], c1[0][:].indirect(idx3[:]), COPY)
-        nc.scalar.activation(looked1[:], c1[1][:].indirect(entries(idx3, 0, HALF)), COPY)
-        nc.vector.tensor_tensor(res1b[:], c1[1][:].indirect(entries(idx3, HALF, HALF)), o_late[:, 1, :], SUBTRACT)
-        nc.sync.dma_start(out[P:, HALF:], res1b[:])
-        nc.vector.tensor_tensor(res0[:, :HALF], looked0[:, :HALF], o_early[:, 0, :], SUBTRACT)
-        nc.vector.tensor_tensor(res0[:, HALF:], looked0[:, HALF:], o_late[:, 0, :], SUBTRACT)
-        nc.sync.dma_start(out[:P, :], res0[:])
-        nc.vector.tensor_tensor(res1a[:], looked1[:], o_early[:, 1, :], SUBTRACT)
-        nc.sync.dma_start(out[P:, :HALF], res1a[:])
+        nc.scalar.activation(looked[0][:], c1[0][:].indirect(entries(idx3, 0, PLAIN)), COPY)
+        nc.scalar.activation(looked[1][:, :HALF], c1[1][:].indirect(entries(idx3, 0, HALF)), COPY)
+        nc.scalar.activation(looked[1][:, HALF:], c1[1][:].indirect(entries(idx3, HALF, CHUNK)), COPY)
+        for h in range(2):
+            nc.vector.tensor_tensor(
+                res[h][:, PLAIN:], c1[h][:].indirect(entries(idx3, PLAIN, CHUNK)), o_late[:, h, CHUNK:], SUBTRACT
+            )
+        for h in range(2):
+            rows = slice(h * P, (h + 1) * P)
+            nc.vector.tensor_tensor(res[h][:, :HALF], looked[h][:, :HALF], o_early[:, h, :], SUBTRACT)
+            nc.sync.dma_start(out[rows, :HALF], res[h][:, :HALF])
+            nc.vector.tensor_tensor(res[h][:, HALF:PLAIN], looked[h][:, HALF:], o_late[:, h, :CHUNK], SUBTRACT)
+            nc.sync.dma_start(out[rows, HALF:], res[h][:, HALF:])

from contextlib import ExitStack

import concourse.mybir as mybir

F32 = mybir.dt.float32
BF16 = mybir.dt.bfloat16
I32 = mybir.dt.int32
U32 = mybir.dt.uint32
U16 = mybir.dt.uint16
U8 = mybir.dt.uint8
FP8X4 = mybir.dt.float8_e4m3fn_x4
FP4X4 = mybir.dt.float4_e2m1fn_x4
COPY = mybir.ActivationFunctionType.Copy
MULT = mybir.AluOpType.mult
ADD = mybir.AluOpType.add
SUBTRACT = mybir.AluOpType.subtract

P = 128
PACK = 4
D, K, T, M, SLOTS, E = 512, 512, 2048, 1024, 512, 256
CHUNK = 128
CHUNKS = SLOTS // CHUNK
HALF = SLOTS // 2
PLAIN = SLOTS - CHUNK
FLOPS = 2 * D * K * SLOTS + 2 * K * E * SLOTS


def entries(offsets, start, count):
    return offsets[:, start // 16 : (start + count) // 16]


def load_scale_rows(queue, tile, rows, quadrants):
    for q in quadrants:
        queue.dma_start(tile[32 * q : 32 * q + 4, :].bitcast(I32), rows[0, 4 * q : 4 * q + 4, :].bitcast(I32))


def tile_attend_outputsback_kernel(tc, pages_words, pages_scales, wa_words, wa_scales, kf, wo_words, wo_scales,
                                    store, offs, offs2, offs3, out):
    nc = tc.nc
    with ExitStack() as ctx:
        sb = ctx.enter_context(tc.tile_pool(name="sb", bufs=1))
        psum = ctx.enter_context(tc.psum_pool(name="psum", bufs=1))

        idx = sb.tile([P, SLOTS // 16], U16, name="idx")
        idx2 = sb.tile([P, SLOTS // 16], U16, name="idx2")
        idx3 = sb.tile([P, SLOTS // 16], U16, name="idx3")
        page_words = sb.tile([P, T], I32, name="page_words", align_bytes=64)
        page_scales = sb.tile([P, T], U8, name="page_scales", align_bytes=64)
        wa_raw = sb.tile([P, 2 * K], U8, name="wa_raw", align_bytes=64)
        wa_raw_scales = sb.tile([P, K], U8, name="wa_raw_scales", tag="staged", align_bytes=64)
        wa_codes = sb.tile([P, 2 * K], U8, name="wa_codes", align_bytes=64)
        wa_plane = sb.tile([P, K], U8, name="wa_plane", align_bytes=64)
        wo_codes = sb.tile([P, 2 * E], U8, name="wo_codes", align_bytes=64)
        wo_plane = sb.tile([P, E], U8, name="wo_plane", align_bytes=64)
        factors = sb.tile([P, 1, PACK], F32, name="factors")
        picked_scales = sb.tile([P, SLOTS], U8, name="picked_scales", align_bytes=64)
        w_codes = sb.tile([P, SLOTS], U32, name="w_codes", align_bytes=64)
        w_plane = sb.tile([P, SLOTS], U8, name="w_plane", align_bytes=64)
        o_early = sb.tile([P, 2, HALF], F32, name="o_early", align_bytes=64)
        o_late = sb.tile([P, 2, HALF], F32, name="o_late", align_bytes=64)
        old = [sb.tile([P, M], F32, name="old%d" % h, align_bytes=64) for h in range(2)]
        placed = [sb.tile([P, M], F32, name="placed%d" % h, align_bytes=64) for h in range(2)]
        looked = [sb.tile([P, PLAIN], F32, name="looked%d" % h, align_bytes=64) for h in range(2)]
        res = [sb.tile([P, SLOTS], F32, name="res%d" % h, align_bytes=64) for h in range(2)]

        nc.vector.memset(page_scales[:].bitcast(I32), 0)
        nc.vector.memset(wa_raw_scales[:].bitcast(I32), 0)
        nc.vector.memset(wo_plane[:].bitcast(I32), 0)
        for h in range(2):
            nc.vector.memset(placed[h][:], 0.0)

        nc.sync.dma_start(idx[:], offs)
        nc.sync.dma_start(wa_raw[:].bitcast(I32), wa_words[0].bitcast(I32))
        load_scale_rows(nc.sync, page_scales, pages_scales, range(4))
        nc.sync.dma_start(page_words[:], pages_words[0].rearrange("p n t -> p (n t)").bitcast(I32))
        nc.sync.dma_start(factors[:], kf.rearrange("(p t) u -> p u t", t=PACK))
        load_scale_rows(nc.sync, wa_raw_scales, wa_scales, range(4))
        nc.sync.dma_start(wo_codes[:].bitcast(I32), wo_words[0].bitcast(I32))
        load_scale_rows(nc.sync, wo_plane, wo_scales, range(4))
        nc.sync.dma_start(idx2[:], offs2)
        for h in range(2):
            nc.sync.dma_start(old[h][:], store[h * P : (h + 1) * P, :])
        nc.sync.dma_start(idx3[:], offs3)

        nc.vector.tensor_copy(
            wa_codes[:].bitcast(U16).rearrange("p (t m) -> p t m", t=PACK),
            wa_raw[:].bitcast(U16).rearrange("p (m t) -> p t m", t=PACK),
        )
        nc.vector.tensor_copy(picked_scales[:], page_scales[:].indirect(idx[:]))
        nc.vector.tensor_copy(
            wa_plane[:].rearrange("p (t m) -> p t m", t=PACK),
            wa_raw_scales[:].rearrange("p (m t) -> p t m", t=PACK),
        )

        picked_first = sb.tile([P, CHUNK], U32, name="picked_first", align_bytes=64)
        picked_rest = sb.tile([P, SLOTS - CHUNK], U32, name="picked_rest", tag="staged", align_bytes=64)
        picked_words = [picked_first[:]] + [picked_rest[:, c * CHUNK : (c + 1) * CHUNK] for c in range(CHUNKS - 1)]
        z = []
        for c in range(CHUNKS):
            cols = slice(c * CHUNK, (c + 1) * CHUNK)
            nc.vector.tensor_copy(picked_words[c], page_words[:].bitcast(U32).indirect(entries(idx, c * CHUNK, CHUNK)))
            bank = psum.tile([P, PACK, CHUNK], F32, name="z%d" % c)
            for t in range(PACK):
                nc.tensor.matmul_mx(
                    bank[:, t, :],
                    lhsT=wa_codes[:, 2 * P * t : 2 * P * (t + 1)].bitcast(FP4X4),
                    lhsT_scale=wa_plane[:, P * t : P * (t + 1)],
                    rhs=picked_words[c].bitcast(FP8X4),
                    rhs_scale=picked_scales[:, cols],
                    start=True,
                    stop=True,
                )
            z.append(bank)

        def output_product(bank, cols):
            for h in range(2):
                nc.tensor.matmul_mx(
                    bank[:, h, :],
                    lhsT=wo_codes[:, 2 * P * h : 2 * P * (h + 1)].bitcast(FP4X4),
                    lhsT_scale=wo_plane[:, P * h : P * (h + 1)],
                    rhs=w_codes[:, cols].bitcast(FP8X4),
                    rhs_scale=w_plane[:, cols],
                    start=True,
                    stop=True,
                )

        for c in range(CHUNKS):
            cols = slice(c * CHUNK, (c + 1) * CHUNK)
            w = sb.tile([P, CHUNK, PACK], BF16, name="w%d" % c, align_bytes=64)
            nc.vector.tensor_tensor(
                w[:], z[c][:].rearrange("p t i -> p i t"), factors[:].to_broadcast([P, CHUNK, PACK]), MULT
            )
            nc.vector.quantize_mx(
                w_codes[:, cols].bitcast(FP8X4), w_plane[:, cols], w[:].rearrange("p i t -> p (i t)")
            )
            if c < 2:
                bank = psum.tile([P, 2, CHUNK], F32, name="o%d" % c)
                output_product(bank, cols)
                nc.scalar.activation(o_early[:, :, cols], bank[:], COPY)
        bank = psum.tile([P, 2, HALF], F32, name="o_late_bank")
        output_product(bank, slice(HALF, SLOTS))

        nc.vector.tensor_copy(placed[0][:].indirect(entries(idx2, 0, HALF)), o_early[:, 0, :])
        nc.scalar.activation(placed[1][:].indirect(entries(idx2, 0, CHUNK)), o_early[:, 1, :CHUNK], COPY)
        nc.scalar.activation(o_late[:], bank[:], COPY)
        nc.vector.tensor_copy(placed[0][:].indirect(entries(idx2, HALF, HALF)), o_late[:, 0, :])
        nc.scalar.activation(placed[1][:].indirect(entries(idx2, HALF, HALF)), o_late[:, 1, :], COPY)
        nc.scalar.activation(placed[1][:].indirect(entries(idx2, CHUNK, CHUNK)), o_early[:, 1, CHUNK:], COPY)

        c1 = []
        for h in range(2):
            c1.append(sb.tile([P, M], F32, name="c1_%d" % h, align_bytes=64))
            nc.vector.tensor_tensor(c1[h][:], old[h][:], placed[h][:], ADD)

        nc.scalar.activation(looked[0][:], c1[0][:].indirect(entries(idx3, 0, PLAIN)), COPY)
        nc.scalar.activation(looked[1][:, :HALF], c1[1][:].indirect(entries(idx3, 0, HALF)), COPY)
        nc.scalar.activation(looked[1][:, HALF:], c1[1][:].indirect(entries(idx3, HALF, CHUNK)), COPY)
        for h in range(2):
            nc.vector.tensor_tensor(
                res[h][:, PLAIN:], c1[h][:].indirect(entries(idx3, PLAIN, CHUNK)), o_late[:, h, CHUNK:], SUBTRACT
            )
        for h in range(2):
            rows = slice(h * P, (h + 1) * P)
            nc.vector.tensor_tensor(res[h][:, :HALF], looked[h][:, :HALF], o_early[:, h, :], SUBTRACT)
            nc.sync.dma_start(out[rows, :HALF], res[h][:, :HALF])
            nc.vector.tensor_tensor(res[h][:, HALF:PLAIN], looked[h][:, HALF:], o_late[:, h, :CHUNK], SUBTRACT)
            nc.sync.dma_start(out[rows, HALF:], res[h][:, HALF:])
